import numpy as np
import ml_dtypes


def mxq(x, axis, fmt="e4m3"):
    dtype, down = {"e4m3": (ml_dtypes.float8_e4m3fn, 7), "e5m2": (ml_dtypes.float8_e5m2, 14)}[fmt]
    v = np.moveaxis(np.asarray(x, np.float32).astype(ml_dtypes.bfloat16).astype(np.float64), axis, -1)
    blocks = v.reshape(v.shape[:-1] + (-1, 32))
    amax = np.abs(blocks).max(-1, keepdims=True)
    byte = np.maximum(np.where(amax > 0, np.frexp(amax)[1] - 1 + 127, 0) - down, 1)
    scale = np.exp2(byte - 127.0)
    codes = (blocks / scale).astype(np.float32).astype(dtype).astype(np.float64)
    return np.moveaxis((codes * scale).reshape(v.shape), -1, axis)


WIDE = False


def mx_kscale(k):
    if not WIDE:
        return np.ones(k)
    levels = np.array([10, -10, 5, -5, 0])
    if k % 512:
        return np.exp2(np.random.permutation(np.resize(levels, k // 32))).repeat(32)
    a = np.empty((k // 512, 16))
    for p in range(k // 512):
        a[p, :8] = np.random.permutation(np.resize(levels, 8))
        for g in range(8):
            far = levels[np.abs(levels - a[p, g]) >= 10]
            a[p, g + 8] = far[np.random.randint(len(far))]
    return np.exp2(a.ravel()).repeat(32)


def f64(x):
    return np.asarray(x).astype(np.float64)


def striped(idx):
    return np.tile(idx.reshape(-1, 16).T, (8, 1)).astype(np.uint16)


def unstriped(offs):
    return offs[:16].T.reshape(-1).astype(np.int64)


E2M1 = np.array([0.0, 0.5, 1.0, 1.5, 2.0, 3.0, 4.0, 6.0, -0.0, -0.5, -1.0, -1.5, -2.0, -3.0, -4.0, -6.0])


def pack_weight(w, fmt):
    k, n = w.shape
    w = f64(np.asarray(w, np.float32).astype(ml_dtypes.bfloat16)).reshape(k // 32, 32, n)
    amax = np.abs(w).max(1)
    if fmt == "e4m3":
        byte = np.frexp(amax)[1] - 1 + 127 - 7
    else:
        mant, ex = np.frexp(amax / 6.0)
        byte = np.where(mant > 0.5, ex, ex - 1) + 127
    byte = np.clip(np.where(amax > 0, byte, 1), 1, 254)
    scaled = (w * np.exp2(127.0 - byte)[:, None, :]).reshape(k, n).astype(np.float32)
    by_word = np.ascontiguousarray(scaled.reshape(k // 512, 128, 4, n).transpose(0, 1, 3, 2))
    if fmt == "e4m3":
        words = by_word.astype(ml_dtypes.float8_e4m3fn).view(np.uint8)
    else:
        c = by_word.astype(ml_dtypes.float4_e2m1fn).view(np.uint8) & 0xF
        words = (c[..., 0::2] | (c[..., 1::2] << 4)).reshape(k // 512, 128, 2 * n)
    return np.ascontiguousarray(words), np.ascontiguousarray(byte.astype(np.uint8).reshape(k // 512, 16, n))


def unpack_weight(words, scales, fmt):
    g, _, n = scales.shape
    words = np.ascontiguousarray(words).reshape(g, 128, n, -1)
    if fmt == "e4m3":
        vals = words.view(ml_dtypes.float8_e4m3fn).astype(np.float64)
    else:
        nib = np.empty((g, 128, n, 4), np.uint8)
        nib[..., 0::2] = words & 0xF
        nib[..., 1::2] = words >> 4
        vals = E2M1[nib]
    vals = vals * np.repeat(np.exp2(scales.astype(np.float64) - 127.0), 8, axis=1)[..., None]
    return vals.transpose(0, 1, 3, 2).reshape(g * 512, n)


def gelu(v):
    return 0.5 * v * (1.0 + np.tanh(np.sqrt(2.0 / np.pi) * (v + 0.044715 * v**3)))


def bf(x):
    return np.asarray(x, np.float32).astype(ml_dtypes.bfloat16)

def planes(Y):
    n, m = Y.shape
    b = f64(bf(Y)).reshape(n // 32, 32, m)
    amax = np.abs(b).max(1)
    byte = np.clip(np.where(amax > 0, np.frexp(amax)[1] - 1 + 127 - 7, 1), 1, 254)
    codes = (b * np.exp2(127.0 - byte)[:, None, :]).reshape(n, m).astype(np.float32).astype(ml_dtypes.float8_e4m3fn).view(np.uint8)
    words = codes.reshape(n // 512, 128, 4, m).transpose(0, 1, 3, 2)
    return np.ascontiguousarray(words), np.ascontiguousarray(byte.astype(np.uint8).reshape(n // 512, 16, m))


K, K2, T, T2, S, H, N = 1024, 512, 4096, 2048, 1024, 1024, 1024

def setup_inputs():
    n = np.random.standard_normal
    s = mx_kscale(K)[:, None]
    s2 = mx_kscale(K2)[:, None]
    u = mx_kscale(H)[:, None]
    tab_words, tab_scales = pack_weight(n((K, T)) * s, "e4m3")
    tab2_words, tab2_scales = pack_weight(n((K2, T2)) * s2, "e4m3")
    w4_words, w4_scales = pack_weight(n((K2, H)) / np.sqrt(K2) / s2 * u.T, "e2m1")
    return {
        "tab_words": tab_words, "tab_scales": tab_scales,
        "tab2_words": tab2_words, "tab2_scales": tab2_scales,
        "offs": striped(np.random.permutation(T)[:S]),
        "offs2": striped(np.random.permutation(T2)[:S]),
        "wl": (n((K, H)) / np.sqrt(K) / s * u.T).astype(np.float32),
        "bl": ((1.0 + 0.3 * n(H)) * u[:, 0]).astype(np.float32),
        "w4_words": w4_words, "w4_scales": w4_scales,
        "bc": ((1.0 + 0.3 * n(H)) * u[:, 0]).astype(np.float32),
        "wy": (n((H, N)) / np.sqrt(H) / u).astype(np.float32),
        "resp": (0.5 * np.exp(0.3 * n(N))).astype(np.float32),
        "area": np.exp(0.8 * n(N)).astype(np.float32),
    }

def reference(tab_words, tab_scales, tab2_words, tab2_scales, offs, offs2, wl, bl, w4_words, w4_scales, bc, wy, resp, area):
    v = unpack_weight(tab_words, tab_scales, "e4m3")[:, unstriped(offs)]
    v2 = unpack_weight(tab2_words, tab2_scales, "e4m3")[:, unstriped(offs2)]
    w4 = unpack_weight(w4_words, w4_scales, "e2m1")
    light = (mxq(f64(wl), 0, "e4m3").T @ v) + f64(bl)[:, None]
    carbon = (w4.T @ v2) + f64(bc)[:, None]
    h = np.minimum(light, carbon)
    p = mxq(f64(wy), 0, "e4m3").T @ mxq(h, 0, "e4m3")
    y = f64(area)[:, None] * (p - f64(resp)[:, None])
    words, scales = planes(y)
    return y, words, scales

@@ -1,0 +1,284 @@
+from contextlib import ExitStack
+
+import concourse.mybir as mybir
+
+K, K2, T, T2, S, H, N = 1024, 512, 4096, 2048, 1024, 1024, 1024
+FLOPS = 2 * S * (K * H + K2 * H + H * N)
+
+F32 = mybir.dt.float32
+BF16 = mybir.dt.bfloat16
+I32 = mybir.dt.int32
+U32 = mybir.dt.uint32
+U16 = mybir.dt.uint16
+U8 = mybir.dt.uint8
+FP8X4 = mybir.dt.float8_e4m3fn_x4
+FP4X4 = mybir.dt.float4_e2m1fn_x4
+ALU = mybir.AluOpType
+IDENTITY = mybir.ActivationFunctionType.Identity
+
+P = 128
+PACK = 4
+PASS = P * PACK
+HALF = 512
+QUADS = 4
+
+
+def tile_list_colimited_canopy_uptake_kernel(
+    tc, tab_words, tab_scales, tab2_words, tab2_scales, offs, offs2, wl, bl,
+    w4_words, w4_scales, bc, wy, resp, area, out_0, out_1, out_2,
+):
+    nc = tc.nc
+    with ExitStack() as ctx:
+        keep = ctx.enter_context(tc.tile_pool(name="keep", bufs=1))
+        raws = ctx.enter_context(tc.tile_pool(name="raws", bufs=6))
+        wide = ctx.enter_context(tc.tile_pool(name="wide", bufs=5))
+        psum = ctx.enter_context(tc.psum_pool(name="psum", bufs=1))
+
+        def held(name, cols, dtype):
+            return keep.tile([P, cols], dtype, name=name, align_bytes=64)
+
+        idx = keep.tile([P, S // 16], U16, name="idx")
+        idx2 = keep.tile([P, S // 16], U16, name="idx2")
+        light_tab = [held("light_tab%d" % a, T, I32) for a in range(2)]
+        light_tab_sc = held("light_tab_sc", T, U8)
+        carbon_tab = held("carbon_tab", T2, I32)
+        carbon_tab_sc = held("carbon_tab_sc", T2, U8)
+        w4_in = held("w4_in", 2 * H, U8)
+        w4_sc_in = held("w4_sc_in", H, U8)
+        w4 = held("w4", 2 * H, U8)
+        w4_sc = held("w4_sc", H, U8)
+        vecs = {}
+        for name in ("bc", "bl", "resp", "area", "shift"):
+            vecs[name] = held("vec_" + name, 2 * PACK, F32)
+
+        half_words = [held("bf16_%d" % i, PACK * HALF, BF16) for i in range(7)]
+        dealt_a, dealt_b, planes_c, woven_d, woven_e, woven_f, woven_g = half_words
+        scalar_banks = [psum.tile([P, HALF], F32, name="scalar_bank%d" % t) for t in range(PACK)]
+        vector_banks = [psum.tile([P, HALF], F32, name="vector_bank%d" % t) for t in range(PACK)]
+
+        nc.vector.memset(w4_sc_in[:].bitcast(I32), 0)
+        nc.vector.memset(carbon_tab_sc[:].bitcast(I32), 0)
+        nc.vector.memset(light_tab_sc[:].bitcast(I32), 0)
+
+        def load_scales(tile, src):
+            for q in range(QUADS):
+                nc.scalar.dma_start(
+                    out=tile[32 * q : 32 * q + 4 * src.shape[0], :].bitcast(I32),
+                    in_=src[:, 4 * q : 4 * q + 4, :].bitcast(I32),
+                )
+
+        def load_words(tile, src):
+            nc.sync.dma_start(out=tile[:], in_=src.rearrange("p t i -> p (t i)").bitcast(I32))
+
+        def load_weight(w, a, g):
+            raw = raws.tile([P, PACK, PASS], F32, name="raw")
+            rows = w[a * PASS : (a + 1) * PASS, g * PASS : (g + 1) * PASS]
+            nc.sync.dma_start(out=raw[:], in_=rows.rearrange("(p j) c -> p j c", j=PACK))
+            return raw
+
+        def load_vec(name, src):
+            nc.sync.dma_start(
+                out=vecs[name][:].rearrange("p (g t) -> p g t", t=PACK),
+                in_=src.rearrange("(g p t) -> p g t", p=P, t=PACK),
+            )
+
+        wl_raw = {}
+        wy_raw = {}
+        load_vec("bc", bc)
+        nc.sync.dma_start(idx2[:], offs2)
+        nc.sync.dma_start(idx[:], offs)
+        nc.sync.dma_start(out=w4_in[:].bitcast(I32), in_=w4_words[0].bitcast(I32))
+        load_scales(w4_sc_in, w4_scales)
+        load_scales(carbon_tab_sc, tab2_scales)
+        load_scales(light_tab_sc, tab_scales)
+        load_words(carbon_tab, tab2_words[0])
+        wl_raw[0, 0] = load_weight(wl, 0, 0)
+        load_words(light_tab[0], tab_words[0])
+        wl_raw[1, 0] = load_weight(wl, 1, 0)
+        load_words(light_tab[1], tab_words[1])
+        load_vec("bl", bl)
+        wl_raw[0, 1] = load_weight(wl, 0, 1)
+        wl_raw[1, 1] = load_weight(wl, 1, 1)
+        load_vec("resp", resp)
+        load_vec("area", area)
+        for g in range(2):
+            for a in range(2):
+                wy_raw[a, g] = load_weight(wy, a, g)
+
+
+        def gather(name, window, offsets, j, dtype):
+            picked = held("%s_%d" % (name, j), HALF, dtype)
+            cols = offsets[:, j * (HALF // 16) : (j + 1) * (HALF // 16)]
+            nc.vector.tensor_copy(picked[:], window[:].bitcast(dtype).indirect(cols))
+            return picked
+
+        def deal_w4_words():
+            nc.vector.tensor_copy(
+                w4[:].bitcast(U16).rearrange("p (g t m) -> p g t m", g=2, t=PACK),
+                w4_in[:].bitcast(U16).rearrange("p (g m t) -> p g t m", g=2, t=PACK),
+            )
+
+        def deal_w4_scales():
+            nc.vector.tensor_copy(
+                w4_sc[:].rearrange("p (g t m) -> p g t m", g=2, t=PACK),
+                w4_sc_in[:].rearrange("p (g m t) -> p g t m", g=2, t=PACK),
+            )
+
+        def copy_on(eng, out, in_):
+            if eng == "vector":
+                nc.vector.tensor_copy(out, in_)
+            else:
+                nc.scalar.copy(out, in_)
+
+        def deal_weight(eng, dealt, raw):
+            copy_on(
+                eng,
+                dealt[:].rearrange("p (t m j) -> p m j t", t=PACK, j=PACK),
+                raw[:].rearrange("p j (m t) -> p m j t", t=PACK),
+            )
+            return dealt
+
+        def weave(eng, woven, planes):
+            copy_on(
+                eng,
+                woven[:].rearrange("p (c i t) -> p c t i", i=4, t=PACK),
+                planes.rearrange("p t (c i) -> p c t i", i=4),
+            )
+            return woven
+
+        def quantize(name, values):
+            codes = held(name, HALF, U32)
+            scales = held(name + "_sc", HALF, U8)
+            nc.vector.quantize_mx(out=codes[:].bitcast(FP8X4), scales=scales[:], in_=values[:])
+            return codes, scales
+
+        def col(name, g, t):
+            return vecs[name][:, g * PACK + t : g * PACK + t + 1]
+
+        carbon = {}
+
+        def carbon_rate(g, j, picked, picked_sc):
+            rate = wide.tile([P, PACK, HALF], F32, name="wide")
+            for t in range(PACK):
+                c0 = g * PASS + t * P
+                acc = scalar_banks[t]
+                nc.tensor.matmul_mx(
+                    out=acc[:],
+                    lhsT=w4[:, 2 * c0 : 2 * (c0 + P)].bitcast(FP4X4),
+                    lhsT_scale=w4_sc[:, c0 : c0 + P],
+                    rhs=picked[:].bitcast(FP8X4),
+                    rhs_scale=picked_sc[:],
+                    start=True,
+                    stop=True,
+                )
+                nc.scalar.activation(rate[:, t, :], acc[:], IDENTITY, bias=col("bc", g, t))
+            carbon[g, j] = rate
+
+        wlq = {}
+        wyq = {}
+        hq = {}
+        v = {}
+        v_sc = {}
+
+        def limit(g, j, tile):
+            planes = tile[:].rearrange("p (t c) -> p t c", t=PACK)
+            for t in range(PACK):
+                acc = vector_banks[t]
+                for a in range(2):
+                    codes, scales = wlq[a, g]
+                    nc.tensor.matmul_mx(
+                        out=acc[:],
+                        lhsT=codes[:, t * P : (t + 1) * P].bitcast(FP8X4),
+                        lhsT_scale=scales[:, t * P : (t + 1) * P],
+                        rhs=v[a, j][:].bitcast(FP8X4),
+                        rhs_scale=v_sc[j][4 * a : P, :],
+                        start=(a == 0),
+                        stop=(a == 1),
+                    )
+                nc.vector.scalar_tensor_tensor(
+                    planes[:, t, :], acc[:], col("bl", g, t), carbon[g, j][:, t, :], ALU.add, ALU.min
+                )
+            return planes
+
+        y_sc = held("y_sc", S, U8)
+
+        def uptake(n, j):
+            y = wide.tile([P, PACK, HALF], F32, name="wide")
+            for t in range(PACK):
+                acc = scalar_banks[t]
+                for g in range(2):
+                    codes, scales = wyq[g, n]
+                    nc.tensor.matmul_mx(
+                        out=acc[:],
+                        lhsT=codes[:, t * P : (t + 1) * P].bitcast(FP8X4),
+                        lhsT_scale=scales[:, t * P : (t + 1) * P],
+                        rhs=hq[g, j][0][:].bitcast(FP8X4),
+                        rhs_scale=hq[g, j][1][:],
+                        start=(g == 0),
+                        stop=(g == 1),
+                    )
+                nc.scalar.activation(
+                    y[:, t, :], acc[:], IDENTITY, bias=col("shift", n, t), scale=col("area", n, t)
+                )
+            rows = out_0[n * PASS : (n + 1) * PASS, j * HALF : (j + 1) * HALF]
+            rows = rows.rearrange("(p t) c -> p t c", t=PACK)
+            for t in range(0, PACK, 2):
+                nc.sync.dma_start(out=rows[:, t : t + 2, :], in_=y[:, t : t + 2, :])
+            return y
+
+        def hand_out_codes(n, j, woven):
+            codes = held("y_codes_%d_%d" % (n, j), HALF, U32)
+            cols = slice(j * HALF, (j + 1) * HALF)
+            nc.vector.quantize_mx(out=codes[:].bitcast(FP8X4), scales=y_sc[4 * n : P, cols], in_=woven[:])
+            words = out_1[n].rearrange("p m t -> p (m t)").bitcast(I32)
+            nc.sync.dma_start(out=words[:, cols], in_=codes[:].bitcast(I32))
+
+        deal_w4_words()
+        deal_w4_scales()
+        v2 = [None, None]
+        for j in range(2):
+            v2[j] = (gather("v2", carbon_tab, idx2, j, U32), gather("v2_sc", carbon_tab_sc, idx2, j, U8))
+        deal_weight("scalar", dealt_a, wl_raw[0, 0])
+        for j in range(2):
+            for g in range(2):
+                carbon_rate(g, j, *v2[j])
+
+        wlq[0, 0] = quantize("wl00", dealt_a)
+        for j in range(2):
+            v_sc[j] = gather("v_sc", light_tab_sc, idx, j, U8)
+        for j in range(2):
+            v[0, j] = gather("v0", light_tab[0], idx, j, U32)
+        wlq[1, 0] = quantize("wl10", deal_weight("vector", dealt_b, wl_raw[1, 0]))
+        for j in range(2):
+            v[1, j] = gather("v1", light_tab[1], idx, j, U32)
+        planes00 = limit(0, 0, planes_c)
+        weave("vector", woven_d, planes00)
+        wlq[0, 1] = quantize("wl01", deal_weight("scalar", dealt_a, wl_raw[0, 1]))
+        wlq[1, 1] = quantize("wl11", deal_weight("scalar", dealt_b, wl_raw[1, 1]))
+        hq[0, 0] = quantize("h00", woven_d)
+        weave("vector", woven_e, limit(1, 0, planes_c))
+        wyq[0, 0] = quantize("wy00", deal_weight("scalar", dealt_a, wy_raw[0, 0]))
+        hq[1, 0] = quantize("h10", woven_e)
+        wyq[1, 0] = quantize("wy10", deal_weight("scalar", dealt_b, wy_raw[1, 0]))
+        deal_weight("scalar", dealt_a, wy_raw[0, 1])
+        nc.vector.scalar_tensor_tensor(
+            vecs["shift"][:], vecs["resp"][:], -1.0, vecs["area"][:], ALU.mult, ALU.mult
+        )
+        y00 = uptake(0, 0)
+        weave("vector", woven_d, limit(0, 1, dealt_b))
+        wyq[0, 1] = quantize("wy01", dealt_a)
+        hq[0, 1] = quantize("h01", woven_d)
+        wyq[1, 1] = quantize("wy11", deal_weight("scalar", dealt_a, wy_raw[1, 1]))
+        weave("vector", woven_e, limit(1, 1, planes_c))
+        hq[1, 1] = quantize("h11", woven_e)
+        y10 = uptake(1, 0)
+        hand_out_codes(0, 0, weave("scalar", woven_f, y00[:]))
+        hand_out_codes(1, 0, weave("vector", woven_g, y10[:]))
+        hand_out_codes(0, 1, weave("vector", woven_f, uptake(0, 1)[:]))
+        hand_out_codes(1, 1, weave("vector", woven_g, uptake(1, 1)[:]))
+        for q in range(QUADS):
+            eng = nc.sync if q % 2 == 0 else nc.scalar
+            eng.dma_start(
+                out=out_2[:, 4 * q : 4 * q + 4, :].bitcast(I32),
+                in_=y_sc[32 * q : 32 * q + 8, :].bitcast(I32),
+            )

@@ -30,8 +30,6 @@ def tile_list_colimited_canopy_uptake_kernel(
     nc = tc.nc
     with ExitStack() as ctx:
         keep = ctx.enter_context(tc.tile_pool(name="keep", bufs=1))
-        raws = ctx.enter_context(tc.tile_pool(name="raws", bufs=6))
-        wide = ctx.enter_context(tc.tile_pool(name="wide", bufs=5))
         psum = ctx.enter_context(tc.psum_pool(name="psum", bufs=1))
 
         def held(name, cols, dtype):
@@ -51,29 +49,32 @@ def tile_list_colimited_canopy_uptake_kernel(
         for name in ("bc", "bl", "resp", "area", "shift"):
             vecs[name] = held("vec_" + name, 2 * PACK, F32)
 
-        half_words = [held("bf16_%d" % i, PACK * HALF, BF16) for i in range(7)]
-        dealt_a, dealt_b, planes_c, woven_d, woven_e, woven_f, woven_g = half_words
+        narrow = [held("narrow%d" % i, PACK * HALF, BF16) for i in range(7)]
+        wide = [held("wide%d" % i, PACK * HALF, F32) for i in range(10)]
         scalar_banks = [psum.tile([P, HALF], F32, name="scalar_bank%d" % t) for t in range(PACK)]
         vector_banks = [psum.tile([P, HALF], F32, name="vector_bank%d" % t) for t in range(PACK)]
 
-        nc.vector.memset(w4_sc_in[:].bitcast(I32), 0)
-        nc.vector.memset(carbon_tab_sc[:].bitcast(I32), 0)
+        nc.gpsimd.memset(w4_sc_in[:].bitcast(I32), 0)
+        nc.gpsimd.memset(carbon_tab_sc[:].bitcast(I32), 0)
         nc.vector.memset(light_tab_sc[:].bitcast(I32), 0)
 
-        def load_scales(tile, src):
-            for q in range(QUADS):
-                nc.scalar.dma_start(
+        def load_scales(eng, tile, src, quads):
+            for q in quads:
+                eng.dma_start(
                     out=tile[32 * q : 32 * q + 4 * src.shape[0], :].bitcast(I32),
                     in_=src[:, 4 * q : 4 * q + 4, :].bitcast(I32),
                 )
 
+        def by_plane(ap):
+            return ap.rearrange("p (t c) -> p t c", t=PACK)
+
         def load_words(tile, src):
             nc.sync.dma_start(out=tile[:], in_=src.rearrange("p t i -> p (t i)").bitcast(I32))
 
-        def load_weight(w, a, g):
-            raw = raws.tile([P, PACK, PASS], F32, name="raw")
+        def load_weight(tile, w, a, g):
+            raw = by_plane(tile[:])
             rows = w[a * PASS : (a + 1) * PASS, g * PASS : (g + 1) * PASS]
-            nc.sync.dma_start(out=raw[:], in_=rows.rearrange("(p j) c -> p j c", j=PACK))
+            nc.sync.dma_start(out=raw, in_=rows.rearrange("(p j) c -> p j c", j=PACK))
             return raw
 
         def load_vec(name, src):
@@ -84,27 +85,26 @@ def tile_list_colimited_canopy_uptake_kernel(
 
         wl_raw = {}
         wy_raw = {}
-        load_vec("bc", bc)
+        load_scales(nc.gpsimd, light_tab_sc, tab_scales, range(4))
         nc.sync.dma_start(idx2[:], offs2)
-        nc.sync.dma_start(idx[:], offs)
         nc.sync.dma_start(out=w4_in[:].bitcast(I32), in_=w4_words[0].bitcast(I32))
-        load_scales(w4_sc_in, w4_scales)
-        load_scales(carbon_tab_sc, tab2_scales)
-        load_scales(light_tab_sc, tab_scales)
+        load_vec("bc", bc)
         load_words(carbon_tab, tab2_words[0])
-        wl_raw[0, 0] = load_weight(wl, 0, 0)
+        load_scales(nc.sync, w4_sc_in, w4_scales, range(4))
+        load_scales(nc.sync, carbon_tab_sc, tab2_scales, range(2))
+        wl_raw[0, 0] = load_weight(wide[0], wl, 0, 0)
+        load_scales(nc.sync, carbon_tab_sc, tab2_scales, range(2, 4))
         load_words(light_tab[0], tab_words[0])
-        wl_raw[1, 0] = load_weight(wl, 1, 0)
-        load_words(light_tab[1], tab_words[1])
+        nc.sync.dma_start(idx[:], offs)
         load_vec("bl", bl)
-        wl_raw[0, 1] = load_weight(wl, 0, 1)
-        wl_raw[1, 1] = load_weight(wl, 1, 1)
         load_vec("resp", resp)
         load_vec("area", area)
-        for g in range(2):
-            for a in range(2):
-                wy_raw[a, g] = load_weight(wy, a, g)
-
+        wl_raw[1, 0] = load_weight(wide[1], wl, 1, 0)
+        load_words(light_tab[1], tab_words[1])
+        wl_raw[0, 1] = load_weight(wide[2], wl, 0, 1)
+        wl_raw[1, 1] = load_weight(wide[3], wl, 1, 1)
+        wy_raw[0, 0] = load_weight(wide[4], wy, 0, 0)
+        wy_raw[1, 0] = load_weight(wide[5], wy, 1, 0)
 
         def gather(name, window, offsets, j, dtype):
             picked = held("%s_%d" % (name, j), HALF, dtype)
@@ -134,22 +134,22 @@ def tile_list_colimited_canopy_uptake_kernel(
             copy_on(
                 eng,
                 dealt[:].rearrange("p (t m j) -> p m j t", t=PACK, j=PACK),
-                raw[:].rearrange("p j (m t) -> p m j t", t=PACK),
+                raw.rearrange("p j (m t) -> p m j t", t=PACK),
             )
-            return dealt
+            return dealt[:]
 
         def weave(eng, woven, planes):
             copy_on(
                 eng,
-                woven[:].rearrange("p (c i t) -> p c t i", i=4, t=PACK),
+                woven.rearrange("p (c i t) -> p c t i", i=4, t=PACK),
                 planes.rearrange("p t (c i) -> p c t i", i=4),
             )
             return woven
 
         def quantize(name, values):
-            codes = held(name, HALF, U32)
-            scales = held(name + "_sc", HALF, U8)
-            nc.vector.quantize_mx(out=codes[:].bitcast(FP8X4), scales=scales[:], in_=values[:])
+            codes = held(name, values.shape[1] // PACK, U32)
+            scales = held(name + "_sc", values.shape[1] // PACK, U8)
+            nc.vector.quantize_mx(out=codes[:].bitcast(FP8X4), scales=scales[:], in_=values)
             return codes, scales
 
         def col(name, g, t):
@@ -158,7 +158,7 @@ def tile_list_colimited_canopy_uptake_kernel(
         carbon = {}
 
         def carbon_rate(g, j, picked, picked_sc):
-            rate = wide.tile([P, PACK, HALF], F32, name="wide")
+            rate = by_plane(wide[6 + 2 * j + g][:])
             for t in range(PACK):
                 c0 = g * PASS + t * P
                 acc = scalar_banks[t]
@@ -180,102 +180,132 @@ def tile_list_colimited_canopy_uptake_kernel(
         v = {}
         v_sc = {}
 
-        def limit(g, j, tile):
-            planes = tile[:].rearrange("p (t c) -> p t c", t=PACK)
+        def limit(g, j, cols, tile):
+            width = cols.stop - cols.start
+            planes = by_plane(tile)
             for t in range(PACK):
-                acc = vector_banks[t]
-                for a in range(2):
+                acc = vector_banks[t][:, 0:width]
+                for a in (1, 0):
                     codes, scales = wlq[a, g]
                     nc.tensor.matmul_mx(
-                        out=acc[:],
+                        out=acc,
                         lhsT=codes[:, t * P : (t + 1) * P].bitcast(FP8X4),
                         lhsT_scale=scales[:, t * P : (t + 1) * P],
-                        rhs=v[a, j][:].bitcast(FP8X4),
-                        rhs_scale=v_sc[j][4 * a : P, :],
-                        start=(a == 0),
-                        stop=(a == 1),
+                        rhs=v[a, j][:, cols].bitcast(FP8X4),
+                        rhs_scale=v_sc[j][4 * a : P, cols],
+                        start=(a == 1),
+                        stop=(a == 0),
                     )
                 nc.vector.scalar_tensor_tensor(
-                    planes[:, t, :], acc[:], col("bl", g, t), carbon[g, j][:, t, :], ALU.add, ALU.min
+                    planes[:, t, :], acc, col("bl", g, t), carbon[g, j][:, t, cols], ALU.add, ALU.min
                 )
             return planes
 
         y_sc = held("y_sc", S, U8)
+        y_codes = [held("y_codes%d" % n, S, U32) for n in range(2)]
 
-        def uptake(n, j):
-            y = wide.tile([P, PACK, HALF], F32, name="wide")
+        def uptake(n, sites, h_parts, tile, planes_a_store):
+            width = sites.stop - sites.start
+            y = by_plane(tile)
+            rows = out_0[n * PASS : (n + 1) * PASS, sites].rearrange("(p t) c -> p t c", t=PACK)
             for t in range(PACK):
-                acc = scalar_banks[t]
+                acc = scalar_banks[t][:, 0:width]
                 for g in range(2):
                     codes, scales = wyq[g, n]
                     nc.tensor.matmul_mx(
-                        out=acc[:],
+                        out=acc,
                         lhsT=codes[:, t * P : (t + 1) * P].bitcast(FP8X4),
                         lhsT_scale=scales[:, t * P : (t + 1) * P],
-                        rhs=hq[g, j][0][:].bitcast(FP8X4),
-                        rhs_scale=hq[g, j][1][:],
+                        rhs=h_parts[g][0].bitcast(FP8X4),
+                        rhs_scale=h_parts[g][1],
                         start=(g == 0),
                         stop=(g == 1),
                     )
                 nc.scalar.activation(
-                    y[:, t, :], acc[:], IDENTITY, bias=col("shift", n, t), scale=col("area", n, t)
+                    y[:, t, :], acc, IDENTITY, bias=col("shift", n, t), scale=col("area", n, t)
                 )
-            rows = out_0[n * PASS : (n + 1) * PASS, j * HALF : (j + 1) * HALF]
-            rows = rows.rearrange("(p t) c -> p t c", t=PACK)
-            for t in range(0, PACK, 2):
-                nc.sync.dma_start(out=rows[:, t : t + 2, :], in_=y[:, t : t + 2, :])
+            for t in range(0, PACK, planes_a_store):
+                nc.sync.dma_start(out=rows[:, t : t + planes_a_store, :], in_=y[:, t : t + planes_a_store, :])
             return y
 
-        def hand_out_codes(n, j, woven):
-            codes = held("y_codes_%d_%d" % (n, j), HALF, U32)
-            cols = slice(j * HALF, (j + 1) * HALF)
-            nc.vector.quantize_mx(out=codes[:].bitcast(FP8X4), scales=y_sc[4 * n : P, cols], in_=woven[:])
+        def quantize_y(n, sites, woven):
+            nc.vector.quantize_mx(
+                out=y_codes[n][:, sites].bitcast(FP8X4), scales=y_sc[4 * n : P, sites], in_=woven
+            )
+
+        def store_codes(n, sites):
             words = out_1[n].rearrange("p m t -> p (m t)").bitcast(I32)
-            nc.sync.dma_start(out=words[:, cols], in_=codes[:].bitcast(I32))
+            nc.sync.dma_start(out=words[:, sites], in_=y_codes[n][:, sites].bitcast(I32))
+
+        whole = slice(0, HALF)
+        quarters = (slice(0, HALF // 2), slice(HALF // 2, HALF))
 
         deal_w4_words()
+        v2 = [gather("v2", carbon_tab, idx2, j, U32) for j in range(2)]
         deal_w4_scales()
-        v2 = [None, None]
-        for j in range(2):
-            v2[j] = (gather("v2", carbon_tab, idx2, j, U32), gather("v2_sc", carbon_tab_sc, idx2, j, U8))
-        deal_weight("scalar", dealt_a, wl_raw[0, 0])
+        v2_sc = [gather("v2_sc", carbon_tab_sc, idx2, j, U8) for j in range(2)]
+        deal_weight("scalar", narrow[0], wl_raw[0, 0])
+        wy_raw[0, 1] = load_weight(wide[0], wy, 0, 1)
         for j in range(2):
             for g in range(2):
-                carbon_rate(g, j, *v2[j])
+                carbon_rate(g, j, v2[j], v2_sc[j])
 
-        wlq[0, 0] = quantize("wl00", dealt_a)
-        for j in range(2):
-            v_sc[j] = gather("v_sc", light_tab_sc, idx, j, U8)
+        wlq[0, 0] = quantize("wl00", narrow[0][:])
         for j in range(2):
             v[0, j] = gather("v0", light_tab[0], idx, j, U32)
-        wlq[1, 0] = quantize("wl10", deal_weight("vector", dealt_b, wl_raw[1, 0]))
         for j in range(2):
-            v[1, j] = gather("v1", light_tab[1], idx, j, U32)
-        planes00 = limit(0, 0, planes_c)
-        weave("vector", woven_d, planes00)
-        wlq[0, 1] = quantize("wl01", deal_weight("scalar", dealt_a, wl_raw[0, 1]))
-        wlq[1, 1] = quantize("wl11", deal_weight("scalar", dealt_b, wl_raw[1, 1]))
-        hq[0, 0] = quantize("h00", woven_d)
-        weave("vector", woven_e, limit(1, 0, planes_c))
-        wyq[0, 0] = quantize("wy00", deal_weight("scalar", dealt_a, wy_raw[0, 0]))
-        hq[1, 0] = quantize("h10", woven_e)
-        wyq[1, 0] = quantize("wy10", deal_weight("scalar", dealt_b, wy_raw[1, 0]))
-        deal_weight("scalar", dealt_a, wy_raw[0, 1])
+            v_sc[j] = gather("v_sc", light_tab_sc, idx, j, U8)
+        wlq[1, 0] = quantize("wl10", deal_weight("vector", narrow[1], wl_raw[1, 0]))
+        wy_raw[1, 1] = load_weight(wide[1], wy, 1, 1)
         nc.vector.scalar_tensor_tensor(
             vecs["shift"][:], vecs["resp"][:], -1.0, vecs["area"][:], ALU.mult, ALU.mult
         )
-        y00 = uptake(0, 0)
-        weave("vector", woven_d, limit(0, 1, dealt_b))
-        wyq[0, 1] = quantize("wy01", dealt_a)
-        hq[0, 1] = quantize("h01", woven_d)
-        wyq[1, 1] = quantize("wy11", deal_weight("scalar", dealt_a, wy_raw[1, 1]))
-        weave("vector", woven_e, limit(1, 1, planes_c))
-        hq[1, 1] = quantize("h11", woven_e)
-        y10 = uptake(1, 0)
-        hand_out_codes(0, 0, weave("scalar", woven_f, y00[:]))
-        hand_out_codes(1, 0, weave("vector", woven_g, y10[:]))
-        hand_out_codes(0, 1, weave("vector", woven_f, uptake(0, 1)[:]))
-        hand_out_codes(1, 1, weave("vector", woven_g, uptake(1, 1)[:]))
+        for j in range(2):
+            v[1, j] = gather("v1", light_tab[1], idx, j, U32)
+        planes00 = limit(0, 0, whole, narrow[4][:])
+        wlq[0, 1] = quantize("wl01", deal_weight("scalar", narrow[2], wl_raw[0, 1]))
+        wlq[1, 1] = quantize("wl11", deal_weight("scalar", narrow[3], wl_raw[1, 1]))
+        hq[0, 0] = quantize("h00", weave("vector", narrow[6][:], planes00))
+        planes01 = limit(0, 1, whole, narrow[3][:])
+        planes10 = limit(1, 0, whole, narrow[4][:])
+        wyq[0, 0] = quantize("wy00", deal_weight("scalar", narrow[0], wy_raw[0, 0]))
+        weave("vector", narrow[6][:], planes10)
+        wyq[1, 0] = quantize("wy10", deal_weight("scalar", narrow[1], wy_raw[1, 0]))
+        hq[1, 0] = quantize("h10", narrow[6][:])
+        deal_weight("scalar", narrow[2], wy_raw[0, 1])
+        deal_weight("scalar", narrow[5], wy_raw[1, 1])
+        h_first = [(hq[g, 0][0][:], hq[g, 0][1][:]) for g in range(2)]
+        y00 = uptake(0, whole, h_first, wide[1][:], 2)
+        wyq[0, 1] = quantize("wy01", narrow[2][:])
+        wyq[1, 1] = quantize("wy11", narrow[5][:])
+        hq[0, 1] = quantize("h01", weave("scalar", narrow[1][:], planes01))
+        h_last = []
+        for k, cols in enumerate(quarters):
+            part = slice(PACK * cols.start, PACK * cols.stop)
+            planes = limit(1, 1, cols, narrow[5][:, part])
+            codes, scales = quantize("h11_%d" % k, weave("vector", narrow[6][:, part], planes))
+            h_last.append([(hq[0, 1][0][:, cols], hq[0, 1][1][:, cols]), (codes[:], scales[:])])
+            if k == 0:
+                y10 = uptake(1, whole, h_first, wide[6][:], 2)
+        y_last = {}
+        for k, cols in enumerate(quarters):
+            part = slice(PACK * cols.start, PACK * cols.stop)
+            sites = slice(HALF + cols.start, HALF + cols.stop)
+            for n in range(2):
+                y_last[k, n] = uptake(n, sites, h_last[k], wide[7 + n][:, part], PACK)
+        weave("vector", narrow[0][:], y00)
+        weave("vector", narrow[1][:], y10)
+        for n in range(2):
+            quantize_y(n, whole, narrow[n][:])
+            store_codes(n, whole)
+        for k, cols in enumerate(quarters):
+            part = slice(PACK * cols.start, PACK * cols.stop)
+            sites = slice(HALF + cols.start, HALF + cols.stop)
+            for n in range(2):
+                eng = "scalar" if (k, n) == (1, 0) else "vector"
+                quantize_y(n, sites, weave(eng, narrow[2 + n][:, part], y_last[k, n]))
+                if k == 1:
+                    store_codes(n, slice(HALF, S))
         for q in range(QUADS):
             eng = nc.sync if q % 2 == 0 else nc.scalar
             eng.dma_start(

@@ -35,6 +35,9 @@ def tile_list_colimited_canopy_uptake_kernel(
         def held(name, cols, dtype):
             return keep.tile([P, cols], dtype, name=name, align_bytes=64)
 
+        def in_turn(slot, name, dtype):
+            return keep.tile([P, PACK * HALF], dtype, name=name, tag=slot, align_bytes=64)
+
         idx = keep.tile([P, S // 16], U16, name="idx")
         idx2 = keep.tile([P, S // 16], U16, name="idx2")
         light_tab = [held("light_tab%d" % a, T, I32) for a in range(2)]
@@ -50,7 +53,7 @@ def tile_list_colimited_canopy_uptake_kernel(
             vecs[name] = held("vec_" + name, 2 * PACK, F32)
 
         narrow = [held("narrow%d" % i, PACK * HALF, BF16) for i in range(7)]
-        wide = [held("wide%d" % i, PACK * HALF, F32) for i in range(10)]
+        wide = [held("wide%d" % i, PACK * HALF, F32) if i != 1 else None for i in range(10)]
         scalar_banks = [psum.tile([P, HALF], F32, name="scalar_bank%d" % t) for t in range(PACK)]
         vector_banks = [psum.tile([P, HALF], F32, name="vector_bank%d" % t) for t in range(PACK)]
 
@@ -58,11 +61,12 @@ def tile_list_colimited_canopy_uptake_kernel(
         nc.gpsimd.memset(carbon_tab_sc[:].bitcast(I32), 0)
         nc.vector.memset(light_tab_sc[:].bitcast(I32), 0)
 
-        def load_scales(eng, tile, src, quads):
+        def load_scales(tile, src, a, quads):
             for q in quads:
-                eng.dma_start(
-                    out=tile[32 * q : 32 * q + 4 * src.shape[0], :].bitcast(I32),
-                    in_=src[:, 4 * q : 4 * q + 4, :].bitcast(I32),
+                row = 32 * q + 4 * a
+                nc.sync.dma_start(
+                    out=tile[row : row + 4, :].bitcast(I32),
+                    in_=src[a, 4 * q : 4 * q + 4, :].bitcast(I32),
                 )
 
         def by_plane(ap):
@@ -85,21 +89,22 @@ def tile_list_colimited_canopy_uptake_kernel(
 
         wl_raw = {}
         wy_raw = {}
-        load_scales(nc.gpsimd, light_tab_sc, tab_scales, range(4))
         nc.sync.dma_start(idx2[:], offs2)
         nc.sync.dma_start(out=w4_in[:].bitcast(I32), in_=w4_words[0].bitcast(I32))
         load_vec("bc", bc)
         load_words(carbon_tab, tab2_words[0])
-        load_scales(nc.sync, w4_sc_in, w4_scales, range(4))
-        load_scales(nc.sync, carbon_tab_sc, tab2_scales, range(2))
+        load_scales(w4_sc_in, w4_scales, 0, range(4))
+        load_scales(carbon_tab_sc, tab2_scales, 0, range(2))
         wl_raw[0, 0] = load_weight(wide[0], wl, 0, 0)
-        load_scales(nc.sync, carbon_tab_sc, tab2_scales, range(2, 4))
+        load_scales(carbon_tab_sc, tab2_scales, 0, range(2, 4))
         load_words(light_tab[0], tab_words[0])
         nc.sync.dma_start(idx[:], offs)
         load_vec("bl", bl)
+        load_scales(light_tab_sc, tab_scales, 0, range(4))
+        wl_raw[1, 0] = load_weight(in_turn("slot_a", "wl10_raw", F32), wl, 1, 0)
+        load_scales(light_tab_sc, tab_scales, 1, range(4))
         load_vec("resp", resp)
         load_vec("area", area)
-        wl_raw[1, 0] = load_weight(wide[1], wl, 1, 0)
         load_words(light_tab[1], tab_words[1])
         wl_raw[0, 1] = load_weight(wide[2], wl, 0, 1)
         wl_raw[1, 1] = load_weight(wide[3], wl, 1, 1)
@@ -253,10 +258,10 @@ def tile_list_colimited_canopy_uptake_kernel(
         wlq[0, 0] = quantize("wl00", narrow[0][:])
         for j in range(2):
             v[0, j] = gather("v0", light_tab[0], idx, j, U32)
+        wlq[1, 0] = quantize("wl10", deal_weight("vector", narrow[1], wl_raw[1, 0]))
         for j in range(2):
             v_sc[j] = gather("v_sc", light_tab_sc, idx, j, U8)
-        wlq[1, 0] = quantize("wl10", deal_weight("vector", narrow[1], wl_raw[1, 0]))
-        wy_raw[1, 1] = load_weight(wide[1], wy, 1, 1)
+        wy_raw[1, 1] = load_weight(in_turn("slot_a", "wy11_raw", F32), wy, 1, 1)
         nc.vector.scalar_tensor_tensor(
             vecs["shift"][:], vecs["resp"][:], -1.0, vecs["area"][:], ALU.mult, ALU.mult
         )
@@ -264,9 +269,9 @@ def tile_list_colimited_canopy_uptake_kernel(
             v[1, j] = gather("v1", light_tab[1], idx, j, U32)
         planes00 = limit(0, 0, whole, narrow[4][:])
         wlq[0, 1] = quantize("wl01", deal_weight("scalar", narrow[2], wl_raw[0, 1]))
-        wlq[1, 1] = quantize("wl11", deal_weight("scalar", narrow[3], wl_raw[1, 1]))
+        wlq[1, 1] = quantize("wl11", deal_weight("scalar", in_turn("slot_b", "wl11_dealt", BF16), wl_raw[1, 1]))
         hq[0, 0] = quantize("h00", weave("vector", narrow[6][:], planes00))
-        planes01 = limit(0, 1, whole, narrow[3][:])
+        planes01 = limit(0, 1, whole, in_turn("slot_b", "planes01", BF16)[:])
         planes10 = limit(1, 0, whole, narrow[4][:])
         wyq[0, 0] = quantize("wy00", deal_weight("scalar", narrow[0], wy_raw[0, 0]))
         weave("vector", narrow[6][:], planes10)
@@ -274,11 +279,12 @@ def tile_list_colimited_canopy_uptake_kernel(
         hq[1, 0] = quantize("h10", narrow[6][:])
         deal_weight("scalar", narrow[2], wy_raw[0, 1])
         deal_weight("scalar", narrow[5], wy_raw[1, 1])
+        woven01 = weave("scalar", in_turn("slot_a", "woven01", BF16)[:], planes01)
         h_first = [(hq[g, 0][0][:], hq[g, 0][1][:]) for g in range(2)]
-        y00 = uptake(0, whole, h_first, wide[1][:], 2)
+        y00 = uptake(0, whole, h_first, in_turn("slot_b", "y00", F32)[:], 2)
         wyq[0, 1] = quantize("wy01", narrow[2][:])
         wyq[1, 1] = quantize("wy11", narrow[5][:])
-        hq[0, 1] = quantize("h01", weave("scalar", narrow[1][:], planes01))
+        hq[0, 1] = quantize("h01", woven01)
         h_last = []
         for k, cols in enumerate(quarters):
             part = slice(PACK * cols.start, PACK * cols.stop)

@@ -138,8 +138,8 @@ def tile_list_colimited_canopy_uptake_kernel(
         def deal_weight(eng, dealt, raw):
             copy_on(
                 eng,
-                dealt[:].rearrange("p (t m j) -> p m j t", t=PACK, j=PACK),
-                raw.rearrange("p j (m t) -> p m j t", t=PACK),
+                dealt[:].rearrange("p (u e m j) -> p u m j e", u=2, e=2, j=PACK),
+                raw.rearrange("p j (m u e) -> p u m j e", u=2, e=2),
             )
             return dealt[:]
 

@@ -20,7 +20,11 @@ P = 128
 PACK = 4
 PASS = P * PACK
 HALF = 512
-QUADS = 4
+QUAD = 32
+GROUP = 16
+VEC_PITCH = 8
+LIGHT_SCALE_ROW = (4, 8)
+Y_SCALE_ROW = (0, 4)
 
 
 def tile_list_colimited_canopy_uptake_kernel(
@@ -35,11 +39,8 @@ def tile_list_colimited_canopy_uptake_kernel(
         def held(name, cols, dtype):
             return keep.tile([P, cols], dtype, name=name, align_bytes=64)
 
-        def in_turn(slot, name, dtype):
-            return keep.tile([P, PACK * HALF], dtype, name=name, tag=slot, align_bytes=64)
-
-        idx = keep.tile([P, S // 16], U16, name="idx")
-        idx2 = keep.tile([P, S // 16], U16, name="idx2")
+        idx = keep.tile([P, S // GROUP], U16, name="idx")
+        idx2 = keep.tile([P, S // GROUP], U16, name="idx2")
         light_tab = [held("light_tab%d" % a, T, I32) for a in range(2)]
         light_tab_sc = held("light_tab_sc", T, U8)
         carbon_tab = held("carbon_tab", T2, I32)
@@ -50,104 +51,90 @@ def tile_list_colimited_canopy_uptake_kernel(
         w4_sc = held("w4_sc", H, U8)
         vecs = {}
         for name in ("bc", "bl", "resp", "area", "shift"):
-            vecs[name] = held("vec_" + name, 2 * PACK, F32)
+            padded = held("vec_" + name, 2 * VEC_PITCH, F32)
+            vecs[name] = padded[:].rearrange("p (g i) -> p g i", i=VEC_PITCH)[:, :, 0:PACK]
 
-        narrow = [held("narrow%d" % i, PACK * HALF, BF16) for i in range(7)]
-        wide = [held("wide%d" % i, PACK * HALF, F32) if i != 1 else None for i in range(10)]
-        scalar_banks = [psum.tile([P, HALF], F32, name="scalar_bank%d" % t) for t in range(PACK)]
-        vector_banks = [psum.tile([P, HALF], F32, name="vector_bank%d" % t) for t in range(PACK)]
+        narrow = [held("narrow%d" % i, PACK * HALF, BF16) for i in range(8)]
+        raw_tiles = [held("raw%d" % i, PACK * PASS, F32) for i in range(6)]
+        carbon_tiles = [held("carbon%d" % i, PACK * HALF, F32) for i in range(4)]
+        scalar_banks = [psum.tile([P, HALF], F32, name="scalar_bank%d" % i) for i in range(PACK)]
+        vector_banks = [psum.tile([P, HALF], F32, name="vector_bank%d" % i) for i in range(PACK)]
 
         nc.gpsimd.memset(w4_sc_in[:].bitcast(I32), 0)
         nc.gpsimd.memset(carbon_tab_sc[:].bitcast(I32), 0)
         nc.vector.memset(light_tab_sc[:].bitcast(I32), 0)
 
-        def load_scales(tile, src, a, quads):
-            for q in quads:
-                row = 32 * q + 4 * a
-                nc.sync.dma_start(
-                    out=tile[row : row + 4, :].bitcast(I32),
-                    in_=src[a, 4 * q : 4 * q + 4, :].bitcast(I32),
-                )
-
         def by_plane(ap):
-            return ap.rearrange("p (t c) -> p t c", t=PACK)
+            return ap.rearrange("p (i c) -> p i c", i=PACK)
+
+        def load_scale_rows(tile, src, rows):
+            by_row = src[0].rearrange("(q s) c -> s q c", s=PACK)
+            for s in rows:
+                nc.sync.dma_start(out=tile[s:P:QUAD, :].bitcast(I32), in_=by_row[s].bitcast(I32))
 
         def load_words(tile, src):
-            nc.sync.dma_start(out=tile[:], in_=src.rearrange("p t i -> p (t i)").bitcast(I32))
+            nc.sync.dma_start(out=tile[:], in_=src.rearrange("p t b -> p (t b)").bitcast(I32))
 
         def load_weight(tile, w, a, g):
-            raw = by_plane(tile[:])
-            rows = w[a * PASS : (a + 1) * PASS, g * PASS : (g + 1) * PASS]
-            nc.sync.dma_start(out=raw, in_=rows.rearrange("(p j) c -> p j c", j=PACK))
+            raw = tile[:].rearrange("p (e c) -> p e c", e=PACK)
+            block = w[a * PASS : (a + 1) * PASS, g * PASS : (g + 1) * PASS]
+            nc.sync.dma_start(out=raw, in_=block.rearrange("(p e) c -> p e c", e=PACK))
             return raw
 
         def load_vec(name, src):
-            nc.sync.dma_start(
-                out=vecs[name][:].rearrange("p (g t) -> p g t", t=PACK),
-                in_=src.rearrange("(g p t) -> p g t", p=P, t=PACK),
-            )
+            nc.sync.dma_start(out=vecs[name], in_=src.rearrange("(g p i) -> p g i", p=P, i=PACK))
 
+        for q in range(P // QUAD):
+            first = QUAD * q + LIGHT_SCALE_ROW[0]
+            nc.gpsimd.dma_start(
+                out=light_tab_sc[first : first + 2 * PACK, :].bitcast(I32),
+                in_=tab_scales[:, PACK * q : PACK * (q + 1), :].bitcast(I32),
+            )
         wl_raw = {}
         wy_raw = {}
         nc.sync.dma_start(idx2[:], offs2)
         nc.sync.dma_start(out=w4_in[:].bitcast(I32), in_=w4_words[0].bitcast(I32))
         load_vec("bc", bc)
         load_words(carbon_tab, tab2_words[0])
-        load_scales(w4_sc_in, w4_scales, 0, range(4))
-        load_scales(carbon_tab_sc, tab2_scales, 0, range(2))
-        wl_raw[0, 0] = load_weight(wide[0], wl, 0, 0)
-        load_scales(carbon_tab_sc, tab2_scales, 0, range(2, 4))
+        load_scale_rows(w4_sc_in, w4_scales, range(PACK))
+        load_scale_rows(carbon_tab_sc, tab2_scales, range(PACK // 2))
+        wl_raw[0, 0] = load_weight(raw_tiles[0], wl, 0, 0)
+        load_scale_rows(carbon_tab_sc, tab2_scales, range(PACK // 2, PACK))
         load_words(light_tab[0], tab_words[0])
         nc.sync.dma_start(idx[:], offs)
         load_vec("bl", bl)
-        load_scales(light_tab_sc, tab_scales, 0, range(4))
-        wl_raw[1, 0] = load_weight(in_turn("slot_a", "wl10_raw", F32), wl, 1, 0)
-        load_scales(light_tab_sc, tab_scales, 1, range(4))
         load_vec("resp", resp)
         load_vec("area", area)
+        wl_raw[1, 0] = load_weight(raw_tiles[1], wl, 1, 0)
         load_words(light_tab[1], tab_words[1])
-        wl_raw[0, 1] = load_weight(wide[2], wl, 0, 1)
-        wl_raw[1, 1] = load_weight(wide[3], wl, 1, 1)
-        wy_raw[0, 0] = load_weight(wide[4], wy, 0, 0)
-        wy_raw[1, 0] = load_weight(wide[5], wy, 1, 0)
+        wl_raw[0, 1] = load_weight(raw_tiles[2], wl, 0, 1)
+        wl_raw[1, 1] = load_weight(raw_tiles[3], wl, 1, 1)
+        wy_raw[0, 0] = load_weight(raw_tiles[4], wy, 0, 0)
+        wy_raw[1, 0] = load_weight(raw_tiles[5], wy, 1, 0)
 
         def gather(name, window, offsets, j, dtype):
             picked = held("%s_%d" % (name, j), HALF, dtype)
-            cols = offsets[:, j * (HALF // 16) : (j + 1) * (HALF // 16)]
-            nc.vector.tensor_copy(picked[:], window[:].bitcast(dtype).indirect(cols))
+            entries = offsets[:, j * (HALF // GROUP) : (j + 1) * (HALF // GROUP)]
+            nc.vector.tensor_copy(picked[:], window[:].bitcast(dtype).indirect(entries))
             return picked
 
-        def deal_w4_words():
+        def deal_packed(dealt, packed):
             nc.vector.tensor_copy(
-                w4[:].bitcast(U16).rearrange("p (g t m) -> p g t m", g=2, t=PACK),
-                w4_in[:].bitcast(U16).rearrange("p (g m t) -> p g t m", g=2, t=PACK),
+                dealt.rearrange("p (g i m) -> p g i m", g=2, i=PACK),
+                packed.rearrange("p (g m i) -> p g i m", g=2, i=PACK),
             )
 
-        def deal_w4_scales():
-            nc.vector.tensor_copy(
-                w4_sc[:].rearrange("p (g t m) -> p g t m", g=2, t=PACK),
-                w4_sc_in[:].rearrange("p (g m t) -> p g t m", g=2, t=PACK),
+        def deal_weight(copy, tile, raw):
+            copy(
+                tile[:].rearrange("p (u d m e) -> p u m e d", u=2, d=2, e=PACK),
+                raw.rearrange("p e (m u d) -> p u m e d", u=2, d=2),
             )
+            return tile[:]
 
-        def copy_on(eng, out, in_):
-            if eng == "vector":
-                nc.vector.tensor_copy(out, in_)
-            else:
-                nc.scalar.copy(out, in_)
-
-        def deal_weight(eng, dealt, raw):
-            copy_on(
-                eng,
-                dealt[:].rearrange("p (u e m j) -> p u m j e", u=2, e=2, j=PACK),
-                raw.rearrange("p j (m u e) -> p u m j e", u=2, e=2),
-            )
-            return dealt[:]
-
-        def weave(eng, woven, planes):
-            copy_on(
-                eng,
-                woven.rearrange("p (c i t) -> p c t i", i=4, t=PACK),
-                planes.rearrange("p t (c i) -> p c t i", i=4),
+        def weave(copy, woven, planes):
+            copy(
+                woven.rearrange("p (c x i) -> p c i x", x=4, i=PACK),
+                planes.rearrange("p i (c x) -> p c i x", x=4),
             )
             return woven
 
@@ -157,150 +144,148 @@ def tile_list_colimited_canopy_uptake_kernel(
             nc.vector.quantize_mx(out=codes[:].bitcast(FP8X4), scales=scales[:], in_=values)
             return codes, scales
 
-        def col(name, g, t):
-            return vecs[name][:, g * PACK + t : g * PACK + t + 1]
+        def col(name, g, i):
+            return vecs[name][:, g, i : i + 1]
 
+        on_vector = nc.vector.tensor_copy
+        on_scalar = nc.scalar.copy
         carbon = {}
-
-        def carbon_rate(g, j, picked, picked_sc):
-            rate = by_plane(wide[6 + 2 * j + g][:])
-            for t in range(PACK):
-                c0 = g * PASS + t * P
-                acc = scalar_banks[t]
-                nc.tensor.matmul_mx(
-                    out=acc[:],
-                    lhsT=w4[:, 2 * c0 : 2 * (c0 + P)].bitcast(FP4X4),
-                    lhsT_scale=w4_sc[:, c0 : c0 + P],
-                    rhs=picked[:].bitcast(FP8X4),
-                    rhs_scale=picked_sc[:],
-                    start=True,
-                    stop=True,
-                )
-                nc.scalar.activation(rate[:, t, :], acc[:], IDENTITY, bias=col("bc", g, t))
-            carbon[g, j] = rate
-
         wlq = {}
         wyq = {}
         hq = {}
         v = {}
-        v_sc = {}
 
-        def limit(g, j, cols, tile):
-            width = cols.stop - cols.start
-            planes = by_plane(tile)
-            for t in range(PACK):
-                acc = vector_banks[t][:, 0:width]
+        def carbon_rate(g, j):
+            rate = by_plane(carbon_tiles[2 * j + g][:])
+            for i in range(PACK):
+                first = g * PASS + i * P
+                nc.tensor.matmul_mx(
+                    out=scalar_banks[i][:],
+                    lhsT=w4[:, 2 * first : 2 * (first + P)].bitcast(FP4X4),
+                    lhsT_scale=w4_sc[:, first : first + P],
+                    rhs=v2[j][:].bitcast(FP8X4),
+                    rhs_scale=v2_sc[j][:],
+                    start=True,
+                    stop=True,
+                )
+                nc.scalar.activation(rate[:, i, :], scalar_banks[i][:], IDENTITY, bias=col("bc", g, i))
+            carbon[g, j] = rate
+
+        def limit(g, j, cols, room):
+            planes = by_plane(room)
+            for i in range(PACK):
+                acc = vector_banks[i][:, 0 : cols.stop - cols.start]
                 for a in (1, 0):
                     codes, scales = wlq[a, g]
                     nc.tensor.matmul_mx(
                         out=acc,
-                        lhsT=codes[:, t * P : (t + 1) * P].bitcast(FP8X4),
-                        lhsT_scale=scales[:, t * P : (t + 1) * P],
+                        lhsT=codes[:, i * P : (i + 1) * P].bitcast(FP8X4),
+                        lhsT_scale=scales[:, i * P : (i + 1) * P],
                         rhs=v[a, j][:, cols].bitcast(FP8X4),
-                        rhs_scale=v_sc[j][4 * a : P, cols],
+                        rhs_scale=v_sc[j][LIGHT_SCALE_ROW[a] : P, cols],
                         start=(a == 1),
                         stop=(a == 0),
                     )
                 nc.vector.scalar_tensor_tensor(
-                    planes[:, t, :], acc, col("bl", g, t), carbon[g, j][:, t, cols], ALU.add, ALU.min
+                    planes[:, i, :], acc, col("bl", g, i), carbon[g, j][:, i, cols], ALU.add, ALU.min
                 )
             return planes
 
         y_sc = held("y_sc", S, U8)
         y_codes = [held("y_codes%d" % n, S, U32) for n in range(2)]
 
-        def uptake(n, sites, h_parts, tile, planes_a_store):
-            width = sites.stop - sites.start
-            y = by_plane(tile)
-            rows = out_0[n * PASS : (n + 1) * PASS, sites].rearrange("(p t) c -> p t c", t=PACK)
-            for t in range(PACK):
-                acc = scalar_banks[t][:, 0:width]
+        def uptake(n, sites, h_parts, room, planes_a_store):
+            y = by_plane(room)
+            rows = out_0[n * PASS : (n + 1) * PASS, sites].rearrange("(p i) c -> p i c", i=PACK)
+            for i in range(PACK):
+                acc = scalar_banks[i][:, 0 : sites.stop - sites.start]
                 for g in range(2):
                     codes, scales = wyq[g, n]
+                    h_codes, h_scales = h_parts[g]
                     nc.tensor.matmul_mx(
                         out=acc,
-                        lhsT=codes[:, t * P : (t + 1) * P].bitcast(FP8X4),
-                        lhsT_scale=scales[:, t * P : (t + 1) * P],
-                        rhs=h_parts[g][0].bitcast(FP8X4),
-                        rhs_scale=h_parts[g][1],
+                        lhsT=codes[:, i * P : (i + 1) * P].bitcast(FP8X4),
+                        lhsT_scale=scales[:, i * P : (i + 1) * P],
+                        rhs=h_codes.bitcast(FP8X4),
+                        rhs_scale=h_scales,
                         start=(g == 0),
                         stop=(g == 1),
                     )
                 nc.scalar.activation(
-                    y[:, t, :], acc, IDENTITY, bias=col("shift", n, t), scale=col("area", n, t)
+                    y[:, i, :], acc, IDENTITY, bias=col("shift", n, i), scale=col("area", n, i)
                 )
-            for t in range(0, PACK, planes_a_store):
-                nc.sync.dma_start(out=rows[:, t : t + planes_a_store, :], in_=y[:, t : t + planes_a_store, :])
+            for i in range(0, PACK, planes_a_store):
+                nc.sync.dma_start(out=rows[:, i : i + planes_a_store, :], in_=y[:, i : i + planes_a_store, :])
             return y
 
         def quantize_y(n, sites, woven):
             nc.vector.quantize_mx(
-                out=y_codes[n][:, sites].bitcast(FP8X4), scales=y_sc[4 * n : P, sites], in_=woven
+                out=y_codes[n][:, sites].bitcast(FP8X4), scales=y_sc[Y_SCALE_ROW[n] : P, sites], in_=woven
             )
 
         def store_codes(n, sites):
-            words = out_1[n].rearrange("p m t -> p (m t)").bitcast(I32)
+            words = out_1[n].rearrange("p m b -> p (m b)").bitcast(I32)
             nc.sync.dma_start(out=words[:, sites], in_=y_codes[n][:, sites].bitcast(I32))
 
         whole = slice(0, HALF)
         quarters = (slice(0, HALF // 2), slice(HALF // 2, HALF))
 
-        deal_w4_words()
+        deal_packed(w4[:].bitcast(U16), w4_in[:].bitcast(U16))
         v2 = [gather("v2", carbon_tab, idx2, j, U32) for j in range(2)]
-        deal_w4_scales()
+        deal_packed(w4_sc[:], w4_sc_in[:])
         v2_sc = [gather("v2_sc", carbon_tab_sc, idx2, j, U8) for j in range(2)]
-        deal_weight("scalar", narrow[0], wl_raw[0, 0])
-        wy_raw[0, 1] = load_weight(wide[0], wy, 0, 1)
+        deal_weight(on_scalar, narrow[0], wl_raw[0, 0])
+        wy_raw[0, 1] = load_weight(raw_tiles[0], wy, 0, 1)
         for j in range(2):
             for g in range(2):
-                carbon_rate(g, j, v2[j], v2_sc[j])
+                carbon_rate(g, j)
 
         wlq[0, 0] = quantize("wl00", narrow[0][:])
         for j in range(2):
             v[0, j] = gather("v0", light_tab[0], idx, j, U32)
-        wlq[1, 0] = quantize("wl10", deal_weight("vector", narrow[1], wl_raw[1, 0]))
-        for j in range(2):
-            v_sc[j] = gather("v_sc", light_tab_sc, idx, j, U8)
-        wy_raw[1, 1] = load_weight(in_turn("slot_a", "wy11_raw", F32), wy, 1, 1)
-        nc.vector.scalar_tensor_tensor(
-            vecs["shift"][:], vecs["resp"][:], -1.0, vecs["area"][:], ALU.mult, ALU.mult
-        )
+        wlq[1, 0] = quantize("wl10", deal_weight(on_vector, narrow[1], wl_raw[1, 0]))
+        v_sc = [gather("v_sc", light_tab_sc, idx, j, U8) for j in range(2)]
+        wy_raw[1, 1] = load_weight(raw_tiles[1], wy, 1, 1)
+        nc.vector.scalar_tensor_tensor(vecs["shift"], vecs["resp"], -1.0, vecs["area"], ALU.mult, ALU.mult)
         for j in range(2):
             v[1, j] = gather("v1", light_tab[1], idx, j, U32)
+
         planes00 = limit(0, 0, whole, narrow[4][:])
-        wlq[0, 1] = quantize("wl01", deal_weight("scalar", narrow[2], wl_raw[0, 1]))
-        wlq[1, 1] = quantize("wl11", deal_weight("scalar", in_turn("slot_b", "wl11_dealt", BF16), wl_raw[1, 1]))
-        hq[0, 0] = quantize("h00", weave("vector", narrow[6][:], planes00))
-        planes01 = limit(0, 1, whole, in_turn("slot_b", "planes01", BF16)[:])
+        wlq[0, 1] = quantize("wl01", deal_weight(on_scalar, narrow[2], wl_raw[0, 1]))
+        wlq[1, 1] = quantize("wl11", deal_weight(on_scalar, narrow[7], wl_raw[1, 1]))
+        hq[0, 0] = quantize("h00", weave(on_vector, narrow[6][:], planes00))
+        planes01 = limit(0, 1, whole, narrow[7][:])
         planes10 = limit(1, 0, whole, narrow[4][:])
-        wyq[0, 0] = quantize("wy00", deal_weight("scalar", narrow[0], wy_raw[0, 0]))
-        weave("vector", narrow[6][:], planes10)
-        wyq[1, 0] = quantize("wy10", deal_weight("scalar", narrow[1], wy_raw[1, 0]))
+        wyq[0, 0] = quantize("wy00", deal_weight(on_scalar, narrow[0], wy_raw[0, 0]))
+        weave(on_vector, narrow[6][:], planes10)
+        wyq[1, 0] = quantize("wy10", deal_weight(on_scalar, narrow[1], wy_raw[1, 0]))
         hq[1, 0] = quantize("h10", narrow[6][:])
-        deal_weight("scalar", narrow[2], wy_raw[0, 1])
-        deal_weight("scalar", narrow[5], wy_raw[1, 1])
-        woven01 = weave("scalar", in_turn("slot_a", "woven01", BF16)[:], planes01)
+        deal_weight(on_scalar, narrow[2], wy_raw[0, 1])
+        deal_weight(on_scalar, narrow[5], wy_raw[1, 1])
+
         h_first = [(hq[g, 0][0][:], hq[g, 0][1][:]) for g in range(2)]
-        y00 = uptake(0, whole, h_first, in_turn("slot_b", "y00", F32)[:], 2)
+        y_first = [uptake(0, whole, h_first, raw_tiles[1][:], 2)]
         wyq[0, 1] = quantize("wy01", narrow[2][:])
         wyq[1, 1] = quantize("wy11", narrow[5][:])
-        hq[0, 1] = quantize("h01", woven01)
+        hq[0, 1] = quantize("h01", weave(on_vector, narrow[5][:], planes01))
         h_last = []
         for k, cols in enumerate(quarters):
             part = slice(PACK * cols.start, PACK * cols.stop)
-            planes = limit(1, 1, cols, narrow[5][:, part])
-            codes, scales = quantize("h11_%d" % k, weave("vector", narrow[6][:, part], planes))
+            planes = limit(1, 1, cols, narrow[4][:, part])
+            codes, scales = quantize("h11_%d" % k, weave(on_vector, narrow[6][:, part], planes))
             h_last.append([(hq[0, 1][0][:, cols], hq[0, 1][1][:, cols]), (codes[:], scales[:])])
             if k == 0:
-                y10 = uptake(1, whole, h_first, wide[6][:], 2)
+                y_first.append(uptake(1, whole, h_first, carbon_tiles[0][:], 2))
+
         y_last = {}
         for k, cols in enumerate(quarters):
             part = slice(PACK * cols.start, PACK * cols.stop)
             sites = slice(HALF + cols.start, HALF + cols.stop)
             for n in range(2):
-                y_last[k, n] = uptake(n, sites, h_last[k], wide[7 + n][:, part], PACK)
-        weave("vector", narrow[0][:], y00)
-        weave("vector", narrow[1][:], y10)
+                y_last[k, n] = uptake(n, sites, h_last[k], carbon_tiles[1 + n][:, part], PACK)
+
+        for n in range(2):
+            weave(on_vector, narrow[n][:], y_first[n])
         for n in range(2):
             quantize_y(n, whole, narrow[n][:])
             store_codes(n, whole)
@@ -308,13 +293,13 @@ def tile_list_colimited_canopy_uptake_kernel(
             part = slice(PACK * cols.start, PACK * cols.stop)
             sites = slice(HALF + cols.start, HALF + cols.stop)
             for n in range(2):
-                eng = "scalar" if (k, n) == (1, 0) else "vector"
-                quantize_y(n, sites, weave(eng, narrow[2 + n][:, part], y_last[k, n]))
+                copy = on_scalar if (k, n) == (1, 0) else on_vector
+                quantize_y(n, sites, weave(copy, narrow[2 + n][:, part], y_last[k, n]))
                 if k == 1:
                     store_codes(n, slice(HALF, S))
-        for q in range(QUADS):
-            eng = nc.sync if q % 2 == 0 else nc.scalar
-            eng.dma_start(
-                out=out_2[:, 4 * q : 4 * q + 4, :].bitcast(I32),
-                in_=y_sc[32 * q : 32 * q + 8, :].bitcast(I32),
+        for q in range(P // QUAD):
+            queue = nc.sync if q % 2 == 0 else nc.scalar
+            queue.dma_start(
+                out=out_2[:, PACK * q : PACK * (q + 1), :].bitcast(I32),
+                in_=y_sc[QUAD * q : QUAD * q + 2 * PACK, :].bitcast(I32),
             )

from contextlib import ExitStack

import concourse.mybir as mybir

K, K2, T, T2, S, H, N = 1024, 512, 4096, 2048, 1024, 1024, 1024
FLOPS = 2 * S * (K * H + K2 * H + H * N)

F32 = mybir.dt.float32
BF16 = mybir.dt.bfloat16
I32 = mybir.dt.int32
U32 = mybir.dt.uint32
U16 = mybir.dt.uint16
U8 = mybir.dt.uint8
FP8X4 = mybir.dt.float8_e4m3fn_x4
FP4X4 = mybir.dt.float4_e2m1fn_x4
ALU = mybir.AluOpType
IDENTITY = mybir.ActivationFunctionType.Identity

P = 128
PACK = 4
PASS = P * PACK
HALF = 512
QUAD = 32
GROUP = 16
VEC_PITCH = 8
LIGHT_SCALE_ROW = (4, 8)
Y_SCALE_ROW = (0, 4)


def tile_list_colimited_canopy_uptake_kernel(
    tc, tab_words, tab_scales, tab2_words, tab2_scales, offs, offs2, wl, bl,
    w4_words, w4_scales, bc, wy, resp, area, out_0, out_1, out_2,
):
    nc = tc.nc
    with ExitStack() as ctx:
        keep = ctx.enter_context(tc.tile_pool(name="keep", bufs=1))
        psum = ctx.enter_context(tc.psum_pool(name="psum", bufs=1))

        def held(name, cols, dtype):
            return keep.tile([P, cols], dtype, name=name, align_bytes=64)

        idx = keep.tile([P, S // GROUP], U16, name="idx")
        idx2 = keep.tile([P, S // GROUP], U16, name="idx2")
        light_tab = [held("light_tab%d" % a, T, I32) for a in range(2)]
        light_tab_sc = held("light_tab_sc", T, U8)
        carbon_tab = held("carbon_tab", T2, I32)
        carbon_tab_sc = held("carbon_tab_sc", T2, U8)
        w4_in = held("w4_in", 2 * H, U8)
        w4_sc_in = held("w4_sc_in", H, U8)
        w4 = held("w4", 2 * H, U8)
        w4_sc = held("w4_sc", H, U8)
        vecs = {}
        for name in ("bc", "bl", "resp", "area", "shift"):
            padded = held("vec_" + name, 2 * VEC_PITCH, F32)
            vecs[name] = padded[:].rearrange("p (g i) -> p g i", i=VEC_PITCH)[:, :, 0:PACK]

        narrow = [held("narrow%d" % i, PACK * HALF, BF16) for i in range(8)]
        raw_tiles = [held("raw%d" % i, PACK * PASS, F32) for i in range(6)]
        carbon_tiles = [held("carbon%d" % i, PACK * HALF, F32) for i in range(4)]
        scalar_banks = [psum.tile([P, HALF], F32, name="scalar_bank%d" % i) for i in range(PACK)]
        vector_banks = [psum.tile([P, HALF], F32, name="vector_bank%d" % i) for i in range(PACK)]

        nc.gpsimd.memset(w4_sc_in[:].bitcast(I32), 0)
        nc.gpsimd.memset(carbon_tab_sc[:].bitcast(I32), 0)
        nc.vector.memset(light_tab_sc[:].bitcast(I32), 0)

        def by_plane(ap):
            return ap.rearrange("p (i c) -> p i c", i=PACK)

        def load_scale_rows(tile, src, rows):
            by_row = src[0].rearrange("(q s) c -> s q c", s=PACK)
            for s in rows:
                nc.sync.dma_start(out=tile[s:P:QUAD, :].bitcast(I32), in_=by_row[s].bitcast(I32))

        def load_words(tile, src):
            nc.sync.dma_start(out=tile[:], in_=src.rearrange("p t b -> p (t b)").bitcast(I32))

        def load_weight(tile, w, a, g):
            raw = tile[:].rearrange("p (e c) -> p e c", e=PACK)
            block = w[a * PASS : (a + 1) * PASS, g * PASS : (g + 1) * PASS]
            nc.sync.dma_start(out=raw, in_=block.rearrange("(p e) c -> p e c", e=PACK))
            return raw

        def load_vec(name, src):
            nc.sync.dma_start(out=vecs[name], in_=src.rearrange("(g p i) -> p g i", p=P, i=PACK))

        for q in range(P // QUAD):
            first = QUAD * q + LIGHT_SCALE_ROW[0]
            nc.gpsimd.dma_start(
                out=light_tab_sc[first : first + 2 * PACK, :].bitcast(I32),
                in_=tab_scales[:, PACK * q : PACK * (q + 1), :].bitcast(I32),
            )
        wl_raw = {}
        wy_raw = {}
        nc.sync.dma_start(idx2[:], offs2)
        nc.sync.dma_start(out=w4_in[:].bitcast(I32), in_=w4_words[0].bitcast(I32))
        load_vec("bc", bc)
        load_words(carbon_tab, tab2_words[0])
        load_scale_rows(w4_sc_in, w4_scales, range(PACK))
        load_scale_rows(carbon_tab_sc, tab2_scales, range(PACK // 2))
        wl_raw[0, 0] = load_weight(raw_tiles[0], wl, 0, 0)
        load_scale_rows(carbon_tab_sc, tab2_scales, range(PACK // 2, PACK))
        load_words(light_tab[0], tab_words[0])
        nc.sync.dma_start(idx[:], offs)
        load_vec("bl", bl)
        load_vec("resp", resp)
        load_vec("area", area)
        wl_raw[1, 0] = load_weight(raw_tiles[1], wl, 1, 0)
        load_words(light_tab[1], tab_words[1])
        wl_raw[0, 1] = load_weight(raw_tiles[2], wl, 0, 1)
        wl_raw[1, 1] = load_weight(raw_tiles[3], wl, 1, 1)
        wy_raw[0, 0] = load_weight(raw_tiles[4], wy, 0, 0)
        wy_raw[1, 0] = load_weight(raw_tiles[5], wy, 1, 0)

        def gather(name, window, offsets, j, dtype):
            picked = held("%s_%d" % (name, j), HALF, dtype)
            entries = offsets[:, j * (HALF // GROUP) : (j + 1) * (HALF // GROUP)]
            nc.vector.tensor_copy(picked[:], window[:].bitcast(dtype).indirect(entries))
            return picked

        def deal_packed(dealt, packed):
            nc.vector.tensor_copy(
                dealt.rearrange("p (g i m) -> p g i m", g=2, i=PACK),
                packed.rearrange("p (g m i) -> p g i m", g=2, i=PACK),
            )

        def deal_weight(copy, tile, raw):
            copy(
                tile[:].rearrange("p (u d m e) -> p u m e d", u=2, d=2, e=PACK),
                raw.rearrange("p e (m u d) -> p u m e d", u=2, d=2),
            )
            return tile[:]

        def weave(copy, woven, planes):
            copy(
                woven.rearrange("p (c x i) -> p c i x", x=4, i=PACK),
                planes.rearrange("p i (c x) -> p c i x", x=4),
            )
            return woven

        def quantize(name, values):
            codes = held(name, values.shape[1] // PACK, U32)
            scales = held(name + "_sc", values.shape[1] // PACK, U8)
            nc.vector.quantize_mx(out=codes[:].bitcast(FP8X4), scales=scales[:], in_=values)
            return codes, scales

        def col(name, g, i):
            return vecs[name][:, g, i : i + 1]

        on_vector = nc.vector.tensor_copy
        on_scalar = nc.scalar.copy
        carbon = {}
        wlq = {}
        wyq = {}
        hq = {}
        v = {}

        def carbon_rate(g, j):
            rate = by_plane(carbon_tiles[2 * j + g][:])
            for i in range(PACK):
                first = g * PASS + i * P
                nc.tensor.matmul_mx(
                    out=scalar_banks[i][:],
                    lhsT=w4[:, 2 * first : 2 * (first + P)].bitcast(FP4X4),
                    lhsT_scale=w4_sc[:, first : first + P],
                    rhs=v2[j][:].bitcast(FP8X4),
                    rhs_scale=v2_sc[j][:],
                    start=True,
                    stop=True,
                )
                nc.scalar.activation(rate[:, i, :], scalar_banks[i][:], IDENTITY, bias=col("bc", g, i))
            carbon[g, j] = rate

        def limit(g, j, cols, room):
            planes = by_plane(room)
            for i in range(PACK):
                acc = vector_banks[i][:, 0 : cols.stop - cols.start]
                for a in (1, 0):
                    codes, scales = wlq[a, g]
                    nc.tensor.matmul_mx(
                        out=acc,
                        lhsT=codes[:, i * P : (i + 1) * P].bitcast(FP8X4),
                        lhsT_scale=scales[:, i * P : (i + 1) * P],
                        rhs=v[a, j][:, cols].bitcast(FP8X4),
                        rhs_scale=v_sc[j][LIGHT_SCALE_ROW[a] : P, cols],
                        start=(a == 1),
                        stop=(a == 0),
                    )
                nc.vector.scalar_tensor_tensor(
                    planes[:, i, :], acc, col("bl", g, i), carbon[g, j][:, i, cols], ALU.add, ALU.min
                )
            return planes

        y_sc = held("y_sc", S, U8)
        y_codes = [held("y_codes%d" % n, S, U32) for n in range(2)]

        def uptake(n, sites, h_parts, room, planes_a_store):
            y = by_plane(room)
            rows = out_0[n * PASS : (n + 1) * PASS, sites].rearrange("(p i) c -> p i c", i=PACK)
            for i in range(PACK):
                acc = scalar_banks[i][:, 0 : sites.stop - sites.start]
                for g in range(2):
                    codes, scales = wyq[g, n]
                    h_codes, h_scales = h_parts[g]
                    nc.tensor.matmul_mx(
                        out=acc,
                        lhsT=codes[:, i * P : (i + 1) * P].bitcast(FP8X4),
                        lhsT_scale=scales[:, i * P : (i + 1) * P],
                        rhs=h_codes.bitcast(FP8X4),
                        rhs_scale=h_scales,
                        start=(g == 0),
                        stop=(g == 1),
                    )
                nc.scalar.activation(
                    y[:, i, :], acc, IDENTITY, bias=col("shift", n, i), scale=col("area", n, i)
                )
            for i in range(0, PACK, planes_a_store):
                nc.sync.dma_start(out=rows[:, i : i + planes_a_store, :], in_=y[:, i : i + planes_a_store, :])
            return y

        def quantize_y(n, sites, woven):
            nc.vector.quantize_mx(
                out=y_codes[n][:, sites].bitcast(FP8X4), scales=y_sc[Y_SCALE_ROW[n] : P, sites], in_=woven
            )

        def store_codes(n, sites):
            words = out_1[n].rearrange("p m b -> p (m b)").bitcast(I32)
            nc.sync.dma_start(out=words[:, sites], in_=y_codes[n][:, sites].bitcast(I32))

        whole = slice(0, HALF)
        quarters = (slice(0, HALF // 2), slice(HALF // 2, HALF))

        deal_packed(w4[:].bitcast(U16), w4_in[:].bitcast(U16))
        v2 = [gather("v2", carbon_tab, idx2, j, U32) for j in range(2)]
        deal_packed(w4_sc[:], w4_sc_in[:])
        v2_sc = [gather("v2_sc", carbon_tab_sc, idx2, j, U8) for j in range(2)]
        deal_weight(on_scalar, narrow[0], wl_raw[0, 0])
        wy_raw[0, 1] = load_weight(raw_tiles[0], wy, 0, 1)
        for j in range(2):
            for g in range(2):
                carbon_rate(g, j)

        wlq[0, 0] = quantize("wl00", narrow[0][:])
        for j in range(2):
            v[0, j] = gather("v0", light_tab[0], idx, j, U32)
        wlq[1, 0] = quantize("wl10", deal_weight(on_vector, narrow[1], wl_raw[1, 0]))
        v_sc = [gather("v_sc", light_tab_sc, idx, j, U8) for j in range(2)]
        wy_raw[1, 1] = load_weight(raw_tiles[1], wy, 1, 1)
        nc.vector.scalar_tensor_tensor(vecs["shift"], vecs["resp"], -1.0, vecs["area"], ALU.mult, ALU.mult)
        for j in range(2):
            v[1, j] = gather("v1", light_tab[1], idx, j, U32)

        planes00 = limit(0, 0, whole, narrow[4][:])
        wlq[0, 1] = quantize("wl01", deal_weight(on_scalar, narrow[2], wl_raw[0, 1]))
        wlq[1, 1] = quantize("wl11", deal_weight(on_scalar, narrow[7], wl_raw[1, 1]))
        hq[0, 0] = quantize("h00", weave(on_vector, narrow[6][:], planes00))
        planes01 = limit(0, 1, whole, narrow[7][:])
        planes10 = limit(1, 0, whole, narrow[4][:])
        wyq[0, 0] = quantize("wy00", deal_weight(on_scalar, narrow[0], wy_raw[0, 0]))
        weave(on_vector, narrow[6][:], planes10)
        wyq[1, 0] = quantize("wy10", deal_weight(on_scalar, narrow[1], wy_raw[1, 0]))
        hq[1, 0] = quantize("h10", narrow[6][:])
        deal_weight(on_scalar, narrow[2], wy_raw[0, 1])
        deal_weight(on_scalar, narrow[5], wy_raw[1, 1])

        h_first = [(hq[g, 0][0][:], hq[g, 0][1][:]) for g in range(2)]
        y_first = [uptake(0, whole, h_first, raw_tiles[1][:], 2)]
        wyq[0, 1] = quantize("wy01", narrow[2][:])
        wyq[1, 1] = quantize("wy11", narrow[5][:])
        hq[0, 1] = quantize("h01", weave(on_vector, narrow[5][:], planes01))
        h_last = []
        for k, cols in enumerate(quarters):
            part = slice(PACK * cols.start, PACK * cols.stop)
            planes = limit(1, 1, cols, narrow[4][:, part])
            codes, scales = quantize("h11_%d" % k, weave(on_vector, narrow[6][:, part], planes))
            h_last.append([(hq[0, 1][0][:, cols], hq[0, 1][1][:, cols]), (codes[:], scales[:])])
            if k == 0:
                y_first.append(uptake(1, whole, h_first, carbon_tiles[0][:], 2))

        y_last = {}
        for k, cols in enumerate(quarters):
            part = slice(PACK * cols.start, PACK * cols.stop)
            sites = slice(HALF + cols.start, HALF + cols.stop)
            for n in range(2):
                y_last[k, n] = uptake(n, sites, h_last[k], carbon_tiles[1 + n][:, part], PACK)

        for n in range(2):
            weave(on_vector, narrow[n][:], y_first[n])
        for n in range(2):
            quantize_y(n, whole, narrow[n][:])
            store_codes(n, whole)
        for k, cols in enumerate(quarters):
            part = slice(PACK * cols.start, PACK * cols.stop)
            sites = slice(HALF + cols.start, HALF + cols.stop)
            for n in range(2):
                copy = on_scalar if (k, n) == (1, 0) else on_vector
                quantize_y(n, sites, weave(copy, narrow[2 + n][:, part], y_last[k, n]))
                if k == 1:
                    store_codes(n, slice(HALF, S))
        for q in range(P // QUAD):
            queue = nc.sync if q % 2 == 0 else nc.scalar
            queue.dma_start(
                out=out_2[:, PACK * q : PACK * (q + 1), :].bitcast(I32),
                in_=y_sc[QUAD * q : QUAD * q + 2 * PACK, :].bitcast(I32),
            )
